import numpy as np
import ml_dtypes


def mxq(x, axis, fmt="e4m3"):
    dtype, down = {"e4m3": (ml_dtypes.float8_e4m3fn, 7), "e5m2": (ml_dtypes.float8_e5m2, 14)}[fmt]
    v = np.moveaxis(np.asarray(x, np.float32).astype(ml_dtypes.bfloat16).astype(np.float64), axis, -1)
    blocks = v.reshape(v.shape[:-1] + (-1, 32))
    amax = np.abs(blocks).max(-1, keepdims=True)
    byte = np.maximum(np.where(amax > 0, np.frexp(amax)[1] - 1 + 127, 0) - down, 1)
    scale = np.exp2(byte - 127.0)
    codes = (blocks / scale).astype(np.float32).astype(dtype).astype(np.float64)
    return np.moveaxis((codes * scale).reshape(v.shape), -1, axis)


WIDE = False


def mx_kscale(k, group=512):
    if not WIDE:
        return np.ones(k)
    levels = np.array([10, -10, 5, -5, 0])
    if group != 512:
        return np.exp2(np.random.permutation(np.resize(levels, k // group))).repeat(group)
    if k % 512:
        return np.exp2(np.random.permutation(np.resize(levels, k // 32))).repeat(32)
    a = np.empty((k // 512, 16))
    for p in range(k // 512):
        a[p, :8] = np.random.permutation(np.resize(levels, 8))
        for g in range(8):
            far = levels[np.abs(levels - a[p, g]) >= 10]
            a[p, g + 8] = far[np.random.randint(len(far))]
    return np.exp2(a.ravel()).repeat(32)


def f64(x):
    return np.asarray(x).astype(np.float64)


def striped(idx):
    return np.tile(np.asarray(idx).reshape(-1, 16).T, (8, 1)).astype(np.uint16)


def unstriped(offs):
    return offs[:16].T.reshape(-1).astype(np.int64)


H, KV, D, NQ, N = 2, 2, 256, 512, 512


def setup_inputs():
    n = np.random.standard_normal
    s = mx_kscale(D, 0)[:, None]
    u = mx_kscale(N)
    t = np.random.uniform(0.5, 2.0, N) * u
    v = n((KV, N, 128))
    return {
        "qT": (n((H, D, NQ)) * s * (0.70 / np.sqrt(D))).astype(np.float32),
        "kT": (n((KV, D, N)) / s).astype(np.float32),
        "t": t.reshape(N, 1).astype(np.float32),
        "v": (v / t[:, None]).astype(np.float32),
        "kb": (0.5 * n((N, 1))).astype(np.float32),
        "og": n((H, NQ, 128)).astype(np.float32),
    }


def reference(qT, kT, t, v, kb, og):
    a = mxq(f64(kT), 1, "e4m3").transpose(0, 2, 1) @ mxq(f64(qT), 1, "e4m3")
    a = a + f64(kb)
    p = a / (1.0 + np.exp(-a))
    w = p * f64(t)
    y = mxq(w, 1, "e4m3").transpose(0, 2, 1) @ mxq(f64(v), 1, "e4m3")
    y = y / 16.0
    y = y / (1.0 + np.exp(-f64(og)))
    return y

@@ -1,0 +1,253 @@
+from contextlib import ExitStack
+
+import concourse.mybir as mybir
+
+H, D, NQ, N, E = 2, 256, 512, 512, 128
+FLOPS = 2 * H * N * NQ * D + 2 * H * NQ * N * E
+
+F32 = mybir.dt.float32
+BF16 = mybir.dt.bfloat16
+U32 = mybir.dt.uint32
+U8 = mybir.dt.uint8
+FP8X4 = mybir.dt.float8_e4m3fn_x4
+ACT = mybir.ActivationFunctionType
+ALU = mybir.AluOpType
+
+P = 128
+PACK = 4
+ROWS = D // PACK
+TILE = 128
+RUN = 4
+HALF = P // 2
+CHUNKS = [(0, 128), (128, 256), (384, 128)]
+OUT_SCALE = 1.0 / 32.0
+
+
+def tile_rows_silu_kb_gate_kernel(tc, qT, kT, t, v, kb, og, out):
+    nc = tc.nc
+    with ExitStack() as ctx:
+        sb = ctx.enter_context(tc.tile_pool(name="sb", bufs=1))
+        ps = ctx.enter_context(tc.psum_pool(name="ps", bufs=1))
+        ctx.enter_context(tc.manual_schedule())
+
+        def tile(name, shape, dtype):
+            return sb.tile(shape, dtype, name=name, align_bytes=64)
+
+        warm = tile("warm", [P, 8], F32)
+        t_sb = tile("t_sb", [P, PACK], F32)
+        kb_sb = tile("kb_sb", [P, PACK], F32)
+        k_raw = [tile("k_raw%d" % a, [P, PACK, N // 2], F32) for a in range(2)]
+        k_grp = [[tile("k_grp%d%d" % (a, b), [P, 2, HALF, PACK], BF16) for b in range(2)] for a in range(2)]
+        k_codes = tile("k_codes", [P, PACK, P], U32)
+        k_scales = tile("k_scales", [P, PACK, P], U8)
+        q_raw = [tile("q_raw%d" % c, [P, PACK, w], F32) for c, (q0, w) in enumerate(CHUNKS)]
+        q_grp = [tile("q_grp%d" % c, [P, w, PACK], BF16) for c, (q0, w) in enumerate(CHUNKS)]
+        q_codes = [tile("q_codes%d" % c, [P, w], U32) for c, (q0, w) in enumerate(CHUNKS)]
+        q_scales = [tile("q_scales%d" % c, [P, w], U8) for c, (q0, w) in enumerate(CHUNKS)]
+        v_raw = tile("v_raw", [P, H, PACK, E], F32)
+        v_grp = [tile("v_grp%d" % h, [P, E, PACK], BF16) for h in range(H)]
+        v_codes = [tile("v_codes%d" % h, [P, E], U32) for h in range(H)]
+        v_scales = [tile("v_scales%d" % h, [P, E], U8) for h in range(H)]
+        og_sb = tile("og_sb", [P, H, NQ // TILE, E], F32)
+        gate = tile("gate", [P, H, NQ // TILE, E], F32)
+        units = [(c, h) for c in range(len(CHUNKS)) for h in range(H)]
+        p_sb = {u: tile("p%d%d" % u, [P, PACK, CHUNKS[u[0]][1]], F32) for u in units}
+        w_grp = {u: tile("w_grp%d%d" % u, [P, CHUNKS[u[0]][1], PACK], BF16) for u in units}
+        w_codes = {u: tile("w_codes%d%d" % u, [P, CHUNKS[u[0]][1]], U32) for u in units}
+        w_scales = {u: tile("w_scales%d%d" % u, [P, CHUNKS[u[0]][1]], U8) for u in units}
+        res = {u: tile("res%d%d" % u, [P, CHUNKS[u[0]][1] // TILE, E], F32) for u in units}
+
+        s_ps = [[ps.tile([P, 512], F32, name="s%d%d" % (h, b)) for b in range(3)] for h in range(H)]
+        y_ps = [ps.tile([P, 512], F32, name="y%d" % b) for b in range(2)]
+
+        def score_view(c, h, r):
+            w = CHUNKS[c][1]
+            if w == TILE:
+                return s_ps[h][0][:, r * w : (r + 1) * w]
+            return s_ps[h][1 + r // 2][:, (r % 2) * w : (r % 2 + 1) * w]
+
+        def y_view(c, h):
+            w = CHUNKS[c][1]
+            bank = y_ps[h]
+            q0 = CHUNKS[c][0]
+            return bank[:, q0 : q0 + w]
+
+        def quantize(codes, scales, src):
+            nc.vector.quantize_mx(out=codes.bitcast(FP8X4), scales=scales, in_=src)
+
+        kT_v = kT.rearrange("h (p j) n -> (h p) j n", j=PACK)
+        qT_v = qT.rearrange("h (p j) n -> (h p) j n", j=PACK)
+
+        def load_k(a):
+            nc.sync.dma_start(out=k_raw[a][:], in_=kT_v[:, :, a * (N // 2) : (a + 1) * (N // 2)])
+
+        def load_q(c):
+            q0, w = CHUNKS[c]
+            nc.sync.dma_start(out=q_raw[c][:], in_=qT_v[:, :, q0 : q0 + w])
+
+        load_k(0)
+        nc.scalar.dma_start(out=kb_sb[:], in_=kb.rearrange("(p r) o -> p (r o)", r=PACK))
+        nc.scalar.dma_start(out=t_sb[:], in_=t.rearrange("(p r) o -> p (r o)", r=PACK))
+        load_q(0)
+        load_k(1)
+        load_q(1)
+        nc.sync.dma_start(
+            out=v_raw[:].rearrange("p h r e -> p h (r e)"), in_=v.rearrange("h (p r) e -> p h (r e)", r=PACK)
+        )
+        load_q(2)
+        nc.sync.dma_start(
+            out=og_sb[:].rearrange("p h c e -> p (h c) e"), in_=og.rearrange("h (c p) e -> p (h c) e", p=P)
+        )
+
+        nc.vector.memset(warm[:], 0.0)
+        nc.scalar.activation(out=warm[:, 4:5], in_=warm[:, 0:1], func=ACT.Silu)
+
+        def group_k(a, b, copy):
+            src = k_raw[a][:].rearrange("p j (s r) -> p s j r", r=PACK)[:, :, :, 2 * b : 2 * b + 2]
+            copy(out=k_grp[a][b][:].rearrange("p r s j -> p s j r"), in_=src)
+
+        def quant_k(a, r):
+            cols = slice(a * HALF, (a + 1) * HALF)
+            quantize(k_codes[:, r, cols], k_scales[:, r, cols], k_grp[a][r // 2][:, r % 2].rearrange("p s j -> p (s j)"))
+
+        def group_q(c, copy):
+            copy(
+                out=q_grp[c][:].rearrange("p (c i) j -> p c j i", i=RUN),
+                in_=q_raw[c][:].rearrange("p j (c i) -> p c j i", i=RUN),
+            )
+
+        def quant_q(c):
+            quantize(q_codes[c][:], q_scales[c][:], q_grp[c][:].rearrange("p q j -> p (q j)"))
+
+        def group_v(h):
+            nc.scalar.activation(
+                out=v_grp[h][:].rearrange("p (c i) r -> p c r i", i=RUN),
+                in_=v_raw[:, h].rearrange("p r (c i) -> p c r i", i=RUN),
+                func=ACT.Copy,
+                scale=OUT_SCALE,
+            )
+
+        def quant_v(h):
+            quantize(v_codes[h][:], v_scales[h][:], v_grp[h][:].rearrange("p e r -> p (e r)"))
+
+        def scores(c):
+            w = CHUNKS[c][1]
+            for r in range(PACK):
+                for n0 in range(0, w, TILE):
+                    for h in range(H):
+                        rows = slice(h * ROWS, (h + 1) * ROWS)
+                        nc.tensor.matmul_mx(
+                            out=score_view(c, h, r)[:, n0 : n0 + TILE],
+                            lhsT=k_codes[rows, r, :].bitcast(FP8X4),
+                            lhsT_scale=k_scales[rows, r, :],
+                            rhs=q_codes[c][rows, n0 : n0 + TILE].bitcast(FP8X4),
+                            rhs_scale=q_scales[c][rows, n0 : n0 + TILE],
+                            start=True,
+                            stop=True,
+                        )
+
+        def silu(c, h):
+            for r in range(PACK):
+                nc.scalar.activation(
+                    out=p_sb[(c, h)][:, r], in_=score_view(c, h, r), func=ACT.Silu, bias=kb_sb[:, r : r + 1]
+                )
+
+        def weigh(c, h):
+            w = CHUNKS[c][1]
+            nc.vector.tensor_tensor(
+                out=w_grp[(c, h)][:].rearrange("p (c i) r -> p c r i", i=RUN),
+                in0=p_sb[(c, h)][:].rearrange("p r (c i) -> p c r i", i=RUN),
+                in1=t_sb[:].unsqueeze(1).unsqueeze(3).to_broadcast([P, w // RUN, PACK, RUN]),
+                op=ALU.mult,
+            )
+
+        def quant_w(c, h):
+            u = (c, h)
+            quantize(w_codes[u][:], w_scales[u][:], w_grp[u][:].rearrange("p q r -> p (q r)"))
+
+        def mix(c, h):
+            u = (c, h)
+            for n0 in range(0, CHUNKS[c][1], TILE):
+                nc.tensor.matmul_mx(
+                    out=y_view(c, h)[:, n0 : n0 + TILE],
+                    lhsT=w_codes[u][:, n0 : n0 + TILE].bitcast(FP8X4),
+                    lhsT_scale=w_scales[u][:, n0 : n0 + TILE],
+                    rhs=v_codes[h][:].bitcast(FP8X4),
+                    rhs_scale=v_scales[h][:],
+                    start=True,
+                    stop=True,
+                )
+
+        def half_tanh(c):
+            q0, w = CHUNKS[c]
+            blk = slice(q0 // TILE, (q0 + w) // TILE)
+            nc.scalar.activation(out=gate[:, :, blk], in_=og_sb[:, :, blk], func=ACT.Tanh, scale=0.5)
+
+        def finish(c, h):
+            q0, w = CHUNKS[c]
+            blk = slice(q0 // TILE, (q0 + w) // TILE)
+            nc.vector.scalar_tensor_tensor(
+                out=res[(c, h)][:].rearrange("p b e -> p (b e)"),
+                in0=gate[:, h, blk].rearrange("p b e -> p (b e)"),
+                scalar=1.0,
+                in1=y_view(c, h),
+                op0=ALU.add,
+                op1=ALU.mult,
+            )
+            nc.sync.dma_start(out=out[h, q0 : q0 + w].rearrange("(b p) e -> p b e", p=P), in_=res[(c, h)][:])
+
+        vcopy = nc.vector.tensor_copy
+        scopy = nc.scalar.copy
+
+        group_k(0, 0, vcopy)
+        group_k(0, 1, scopy)
+        group_q(0, vcopy)
+        for r in range(PACK):
+            quant_k(0, r)
+        quant_q(0)
+        group_k(1, 0, vcopy)
+        group_k(1, 1, scopy)
+        for r in range(PACK):
+            quant_k(1, r)
+        scores(0)
+        group_q(1, vcopy)
+        silu(0, 0)
+        quant_q(1)
+        silu(0, 1)
+        scores(1)
+        weigh(0, 0)
+        weigh(0, 1)
+        group_q(2, vcopy)
+        silu(1, 0)
+        quant_w(0, 0)
+        quant_w(0, 1)
+        quant_q(2)
+        scores(2)
+        silu(1, 1)
+        weigh(1, 0)
+        group_v(0)
+        group_v(1)
+        weigh(1, 1)
+        quant_w(1, 0)
+        quant_v(0)
+        quant_v(1)
+        quant_w(1, 1)
+        silu(2, 0)
+        silu(2, 1)
+        for u in units[:4]:
+            mix(*u)
+        half_tanh(0)
+        half_tanh(1)
+        half_tanh(2)
+        weigh(2, 0)
+        weigh(2, 1)
+        quant_w(2, 0)
+        finish(0, 0)
+        quant_w(2, 1)
+        mix(2, 0)
+        mix(2, 1)
+        finish(0, 1)
+        finish(1, 0)
+        finish(1, 1)
+        finish(2, 0)
+        finish(2, 1)

@@ -16,11 +16,13 @@ ALU = mybir.AluOpType
 P = 128
 PACK = 4
 ROWS = D // PACK
-TILE = 128
-RUN = 4
+QC = 128
+CHUNKS = NQ // QC
+RUN = 2
 HALF = P // 2
-CHUNKS = [(0, 128), (128, 256), (384, 128)]
+BANK = 512
 OUT_SCALE = 1.0 / 32.0
+BOTH = slice(0, H)
 
 
 def tile_rows_silu_kb_gate_kernel(tc, qT, kT, t, v, kb, og, out):
@@ -33,6 +35,9 @@ def tile_rows_silu_kb_gate_kernel(tc, qT, kT, t, v, kb, og, out):
         def tile(name, shape, dtype):
             return sb.tile(shape, dtype, name=name, align_bytes=64)
 
+        def per_chunk(name, shape, dtype):
+            return [tile("%s%d" % (name, c), shape, dtype) for c in range(CHUNKS)]
+
         warm = tile("warm", [P, 8], F32)
         t_sb = tile("t_sb", [P, PACK], F32)
         kb_sb = tile("kb_sb", [P, PACK], F32)
@@ -40,37 +45,32 @@ def tile_rows_silu_kb_gate_kernel(tc, qT, kT, t, v, kb, og, out):
         k_grp = [[tile("k_grp%d%d" % (a, b), [P, 2, HALF, PACK], BF16) for b in range(2)] for a in range(2)]
         k_codes = tile("k_codes", [P, PACK, P], U32)
         k_scales = tile("k_scales", [P, PACK, P], U8)
-        q_raw = [tile("q_raw%d" % c, [P, PACK, w], F32) for c, (q0, w) in enumerate(CHUNKS)]
-        q_grp = [tile("q_grp%d" % c, [P, w, PACK], BF16) for c, (q0, w) in enumerate(CHUNKS)]
-        q_codes = [tile("q_codes%d" % c, [P, w], U32) for c, (q0, w) in enumerate(CHUNKS)]
-        q_scales = [tile("q_scales%d" % c, [P, w], U8) for c, (q0, w) in enumerate(CHUNKS)]
+        q_raw = per_chunk("q_raw", [P, PACK, QC], F32)
+        q_grp = per_chunk("q_grp", [P, QC, PACK], BF16)
+        q_codes = per_chunk("q_codes", [P, QC], U32)
+        q_scales = per_chunk("q_scales", [P, QC], U8)
         v_raw = tile("v_raw", [P, H, PACK, E], F32)
-        v_grp = [tile("v_grp%d" % h, [P, E, PACK], BF16) for h in range(H)]
-        v_codes = [tile("v_codes%d" % h, [P, E], U32) for h in range(H)]
-        v_scales = [tile("v_scales%d" % h, [P, E], U8) for h in range(H)]
-        og_sb = tile("og_sb", [P, H, NQ // TILE, E], F32)
-        gate = tile("gate", [P, H, NQ // TILE, E], F32)
-        units = [(c, h) for c in range(len(CHUNKS)) for h in range(H)]
-        p_sb = {u: tile("p%d%d" % u, [P, PACK, CHUNKS[u[0]][1]], F32) for u in units}
-        w_grp = {u: tile("w_grp%d%d" % u, [P, CHUNKS[u[0]][1], PACK], BF16) for u in units}
-        w_codes = {u: tile("w_codes%d%d" % u, [P, CHUNKS[u[0]][1]], U32) for u in units}
-        w_scales = {u: tile("w_scales%d%d" % u, [P, CHUNKS[u[0]][1]], U8) for u in units}
-        res = {u: tile("res%d%d" % u, [P, CHUNKS[u[0]][1] // TILE, E], F32) for u in units}
+        v_grp = tile("v_grp", [P, H, E, PACK], BF16)
+        v_codes = tile("v_codes", [P, H, E], U32)
+        v_scales = tile("v_scales", [P, H, E], U8)
+        og_sb = tile("og_sb", [P, H, CHUNKS, E], F32)
+        gate = per_chunk("gate", [P, H, E], F32)
+        p_sb = per_chunk("p_sb", [P, PACK, H, QC], F32)
+        w_grp = per_chunk("w_grp", [P, H, QC, PACK], BF16)
+        w_codes = per_chunk("w_codes", [P, H, QC], U32)
+        w_scales = per_chunk("w_scales", [P, H, QC], U8)
+        res = per_chunk("res", [P, H, E], F32)
 
-        s_ps = [[ps.tile([P, 512], F32, name="s%d%d" % (h, b)) for b in range(3)] for h in range(H)]
-        y_ps = [ps.tile([P, 512], F32, name="y%d" % b) for b in range(2)]
+        s_ps = [[ps.tile([P, BANK], F32, name="s%d%d" % (h, b)) for b in range(3 - h)] for h in range(H)]
+        y_ps = [ps.tile([P, 2, H, E], F32, name="y%d" % b) for b in range(3)]
+
+        def y_view(c, hs):
+            bank = 2 if (c, hs) == (CHUNKS - 1, slice(0, 1)) else c // 2
+            return y_ps[bank][:, c % 2, hs].rearrange("p h e -> p (h e)")
 
         def score_view(c, h, r):
-            w = CHUNKS[c][1]
-            if w == TILE:
-                return s_ps[h][0][:, r * w : (r + 1) * w]
-            return s_ps[h][1 + r // 2][:, (r % 2) * w : (r % 2 + 1) * w]
-
-        def y_view(c, h):
-            w = CHUNKS[c][1]
-            bank = y_ps[h]
-            q0 = CHUNKS[c][0]
-            return bank[:, q0 : q0 + w]
+            bank = c % 2 if h == 1 else (r // 2 if c == 0 else (c + 1) % 3)
+            return s_ps[h][bank][:, r * QC : (r + 1) * QC]
 
         def quantize(codes, scales, src):
             nc.vector.quantize_mx(out=codes.bitcast(FP8X4), scales=scales, in_=src)
@@ -82,25 +82,21 @@ def tile_rows_silu_kb_gate_kernel(tc, qT, kT, t, v, kb, og, out):
             nc.sync.dma_start(out=k_raw[a][:], in_=kT_v[:, :, a * (N // 2) : (a + 1) * (N // 2)])
 
         def load_q(c):
-            q0, w = CHUNKS[c]
-            nc.sync.dma_start(out=q_raw[c][:], in_=qT_v[:, :, q0 : q0 + w])
+            nc.sync.dma_start(out=q_raw[c][:], in_=qT_v[:, :, c * QC : (c + 1) * QC])
 
-        load_k(0)
-        nc.scalar.dma_start(out=kb_sb[:], in_=kb.rearrange("(p r) o -> p (r o)", r=PACK))
-        nc.scalar.dma_start(out=t_sb[:], in_=t.rearrange("(p r) o -> p (r o)", r=PACK))
-        load_q(0)
-        load_k(1)
-        load_q(1)
-        nc.sync.dma_start(
-            out=v_raw[:].rearrange("p h r e -> p h (r e)"), in_=v.rearrange("h (p r) e -> p h (r e)", r=PACK)
-        )
-        load_q(2)
-        nc.sync.dma_start(
-            out=og_sb[:].rearrange("p h c e -> p (h c) e"), in_=og.rearrange("h (c p) e -> p (h c) e", p=P)
-        )
+        def load_v():
+            nc.sync.dma_start(
+                out=v_raw[:].rearrange("p h r e -> p h (r e)"), in_=v.rearrange("h (p r) e -> p h (r e)", r=PACK)
+            )
 
-        nc.vector.memset(warm[:], 0.0)
-        nc.scalar.activation(out=warm[:, 4:5], in_=warm[:, 0:1], func=ACT.Silu)
+        def load_og():
+            nc.sync.dma_start(
+                out=og_sb[:].rearrange("p h c e -> p (h c) e"), in_=og.rearrange("h (c p) e -> p (h c) e", p=P)
+            )
+
+        def load_small():
+            nc.scalar.dma_start(out=kb_sb[:], in_=kb.rearrange("(p r) o -> p (r o)", r=PACK))
+            nc.scalar.dma_start(out=t_sb[:], in_=t.rearrange("(p r) o -> p (r o)", r=PACK))
 
         def group_k(a, b, copy):
             src = k_raw[a][:].rearrange("p j (s r) -> p s j r", r=PACK)[:, :, :, 2 * b : 2 * b + 2]
@@ -119,135 +115,162 @@ def tile_rows_silu_kb_gate_kernel(tc, qT, kT, t, v, kb, og, out):
         def quant_q(c):
             quantize(q_codes[c][:], q_scales[c][:], q_grp[c][:].rearrange("p q j -> p (q j)"))
 
-        def group_v(h):
-            nc.scalar.activation(
-                out=v_grp[h][:].rearrange("p (c i) r -> p c r i", i=RUN),
-                in_=v_raw[:, h].rearrange("p r (c i) -> p c r i", i=RUN),
-                func=ACT.Copy,
-                scale=OUT_SCALE,
+        def group_v(h, on_vector=False):
+            dst = v_grp[:, h].rearrange("p (c i) r -> p c r i", i=RUN)
+            src = v_raw[:, h].rearrange("p r (c i) -> p c r i", i=RUN)
+            if on_vector:
+                nc.vector.tensor_scalar_mul(out=dst, in0=src, scalar1=OUT_SCALE)
+            else:
+                nc.scalar.activation(out=dst, in_=src, func=ACT.Copy, scale=OUT_SCALE)
+
+        def quant_v(hs):
+            quantize(
+                v_codes[:, hs].rearrange("p h e -> p (h e)"),
+                v_scales[:, hs].rearrange("p h e -> p (h e)"),
+                v_grp[:, hs].rearrange("p h e r -> p (h e r)"),
             )
 
-        def quant_v(h):
-            quantize(v_codes[h][:], v_scales[h][:], v_grp[h][:].rearrange("p e r -> p (e r)"))
-
         def scores(c):
-            w = CHUNKS[c][1]
-            for r in range(PACK):
-                for n0 in range(0, w, TILE):
-                    for h in range(H):
-                        rows = slice(h * ROWS, (h + 1) * ROWS)
-                        nc.tensor.matmul_mx(
-                            out=score_view(c, h, r)[:, n0 : n0 + TILE],
-                            lhsT=k_codes[rows, r, :].bitcast(FP8X4),
-                            lhsT_scale=k_scales[rows, r, :],
-                            rhs=q_codes[c][rows, n0 : n0 + TILE].bitcast(FP8X4),
-                            rhs_scale=q_scales[c][rows, n0 : n0 + TILE],
-                            start=True,
-                            stop=True,
-                        )
+            pairs = [(r, h) for r in range(PACK) for h in range(H)]
+            if c == 0:
+                pairs = [(r, h) for h in range(H) for r in range(PACK)]
+            for r, h in pairs:
+                if True:
+                    rows = slice(h * ROWS, (h + 1) * ROWS)
+                    nc.tensor.matmul_mx(
+                        out=score_view(c, h, r),
+                        lhsT=k_codes[rows, r, :].bitcast(FP8X4),
+                        lhsT_scale=k_scales[rows, r, :],
+                        rhs=q_codes[c][rows, :].bitcast(FP8X4),
+                        rhs_scale=q_scales[c][rows, :],
+                        start=True,
+                        stop=True,
+                    )
 
-        def silu(c, h):
-            for r in range(PACK):
+        def silu(c, h, slots=range(PACK)):
+            for r in slots:
                 nc.scalar.activation(
-                    out=p_sb[(c, h)][:, r], in_=score_view(c, h, r), func=ACT.Silu, bias=kb_sb[:, r : r + 1]
+                    out=p_sb[c][:, r, h], in_=score_view(c, h, r), func=ACT.Silu, bias=kb_sb[:, r : r + 1]
                 )
 
-        def weigh(c, h):
-            w = CHUNKS[c][1]
+        def weigh(c, hs):
+            groups = (hs.stop - hs.start) * QC // RUN
             nc.vector.tensor_tensor(
-                out=w_grp[(c, h)][:].rearrange("p (c i) r -> p c r i", i=RUN),
-                in0=p_sb[(c, h)][:].rearrange("p r (c i) -> p c r i", i=RUN),
-                in1=t_sb[:].unsqueeze(1).unsqueeze(3).to_broadcast([P, w // RUN, PACK, RUN]),
+                out=w_grp[c][:, hs].rearrange("p h (c i) r -> p (h c) r i", i=RUN),
+                in0=p_sb[c][:, :, hs].rearrange("p r h (c i) -> p (h c) r i", i=RUN),
+                in1=t_sb[:].unsqueeze(1).unsqueeze(3).to_broadcast([P, groups, PACK, RUN]),
                 op=ALU.mult,
             )
 
-        def quant_w(c, h):
-            u = (c, h)
-            quantize(w_codes[u][:], w_scales[u][:], w_grp[u][:].rearrange("p q r -> p (q r)"))
+        def quant_w(c, hs):
+            quantize(
+                w_codes[c][:, hs].rearrange("p h q -> p (h q)"),
+                w_scales[c][:, hs].rearrange("p h q -> p (h q)"),
+                w_grp[c][:, hs].rearrange("p h q r -> p (h q r)"),
+            )
 
-        def mix(c, h):
-            u = (c, h)
-            for n0 in range(0, CHUNKS[c][1], TILE):
+        def mix(c, hs):
+            for h in range(hs.start, hs.stop):
                 nc.tensor.matmul_mx(
-                    out=y_view(c, h)[:, n0 : n0 + TILE],
-                    lhsT=w_codes[u][:, n0 : n0 + TILE].bitcast(FP8X4),
-                    lhsT_scale=w_scales[u][:, n0 : n0 + TILE],
-                    rhs=v_codes[h][:].bitcast(FP8X4),
-                    rhs_scale=v_scales[h][:],
+                    out=y_view(c, slice(h, h + 1)),
+                    lhsT=w_codes[c][:, h].bitcast(FP8X4),
+                    lhsT_scale=w_scales[c][:, h],
+                    rhs=v_codes[:, h].bitcast(FP8X4),
+                    rhs_scale=v_scales[:, h],
                     start=True,
                     stop=True,
                 )
 
         def half_tanh(c):
-            q0, w = CHUNKS[c]
-            blk = slice(q0 // TILE, (q0 + w) // TILE)
-            nc.scalar.activation(out=gate[:, :, blk], in_=og_sb[:, :, blk], func=ACT.Tanh, scale=0.5)
+            nc.scalar.activation(out=gate[c][:], in_=og_sb[:, :, c], func=ACT.Tanh, scale=0.5)
 
-        def finish(c, h):
-            q0, w = CHUNKS[c]
-            blk = slice(q0 // TILE, (q0 + w) // TILE)
+        def finish(c, hs):
             nc.vector.scalar_tensor_tensor(
-                out=res[(c, h)][:].rearrange("p b e -> p (b e)"),
-                in0=gate[:, h, blk].rearrange("p b e -> p (b e)"),
+                out=res[c][:, hs].rearrange("p h e -> p (h e)"),
+                in0=gate[c][:, hs].rearrange("p h e -> p (h e)"),
                 scalar=1.0,
-                in1=y_view(c, h),
+                in1=y_view(c, hs),
                 op0=ALU.add,
                 op1=ALU.mult,
             )
-            nc.sync.dma_start(out=out[h, q0 : q0 + w].rearrange("(b p) e -> p b e", p=P), in_=res[(c, h)][:])
+            nc.sync.dma_start(out=out[hs, c * QC : (c + 1) * QC].rearrange("h p e -> p h e"), in_=res[c][:, hs])
 
         vcopy = nc.vector.tensor_copy
         scopy = nc.scalar.copy
+        H0, H1 = slice(0, 1), slice(1, 2)
+
+        load_k(0)
+        load_small()
+        load_q(0)
+        load_k(1)
+        load_q(1)
+        load_q(2)
+        load_q(3)
+        load_v()
+        load_og()
+        nc.vector.memset(warm[:], 0.0)
+        nc.scalar.activation(out=warm[:, 4:5], in_=warm[:, 0:1], func=ACT.Silu)
 
         group_k(0, 0, vcopy)
         group_k(0, 1, scopy)
+        quant_k(0, 0)
+        quant_k(0, 1)
+        quant_k(0, 2)
+        quant_k(0, 3)
         group_q(0, vcopy)
-        for r in range(PACK):
-            quant_k(0, r)
         quant_q(0)
         group_k(1, 0, vcopy)
         group_k(1, 1, scopy)
-        for r in range(PACK):
-            quant_k(1, r)
+        quant_k(1, 0)
+        quant_k(1, 1)
+        quant_k(1, 2)
+        quant_k(1, 3)
         scores(0)
         group_q(1, vcopy)
-        silu(0, 0)
-        quant_q(1)
-        silu(0, 1)
-        scores(1)
-        weigh(0, 0)
-        weigh(0, 1)
         group_q(2, vcopy)
-        silu(1, 0)
-        quant_w(0, 0)
-        quant_w(0, 1)
+        quant_q(1)
+        silu(0, 0)
+        scores(1)
         quant_q(2)
+        group_q(3, vcopy)
+        silu(0, 1)
+        weigh(0, H0)
+        quant_q(3)
         scores(2)
+        silu(1, 0)
         silu(1, 1)
-        weigh(1, 0)
-        group_v(0)
-        group_v(1)
-        weigh(1, 1)
-        quant_w(1, 0)
-        quant_v(0)
-        quant_v(1)
-        quant_w(1, 1)
+        scores(3)
         silu(2, 0)
+        weigh(0, H1)
+        group_v(0, True)
         silu(2, 1)
-        for u in units[:4]:
-            mix(*u)
-        half_tanh(0)
-        half_tanh(1)
+        quant_w(0, BOTH)
+        weigh(1, H0)
+        weigh(1, H1)
+        weigh(2, H0)
+        quant_v(H0)
+        weigh(2, H1)
+        quant_w(1, BOTH)
+        group_v(1)
+        quant_v(H1)
+        mix(0, BOTH)
+        quant_w(2, BOTH)
+        mix(1, BOTH)
+        mix(2, BOTH)
+        silu(3, 0)
+        silu(3, 1)
         half_tanh(2)
-        weigh(2, 0)
-        weigh(2, 1)
-        quant_w(2, 0)
-        finish(0, 0)
-        quant_w(2, 1)
-        mix(2, 0)
-        mix(2, 1)
-        finish(0, 1)
-        finish(1, 0)
-        finish(1, 1)
-        finish(2, 0)
-        finish(2, 1)
+        half_tanh(1)
+        half_tanh(0)
+        half_tanh(3)
+        weigh(3, H0)
+        weigh(3, H1)
+        quant_w(3, H0)
+        mix(3, H0)
+        finish(2, BOTH)
+        quant_w(3, H1)
+        mix(3, H1)
+        finish(1, BOTH)
+        finish(0, BOTH)
+        finish(3, H0)
+        finish(3, H1)

from contextlib import ExitStack

import concourse.mybir as mybir

H, D, NQ, N, E = 2, 256, 512, 512, 128
FLOPS = 2 * H * N * NQ * D + 2 * H * NQ * N * E

F32 = mybir.dt.float32
BF16 = mybir.dt.bfloat16
U32 = mybir.dt.uint32
U8 = mybir.dt.uint8
FP8X4 = mybir.dt.float8_e4m3fn_x4
ACT = mybir.ActivationFunctionType
ALU = mybir.AluOpType

P = 128
PACK = 4
ROWS = D // PACK
QC = 128
CHUNKS = NQ // QC
RUN = 2
HALF = P // 2
BANK = 512
OUT_SCALE = 1.0 / 32.0
BOTH = slice(0, H)


def tile_rows_silu_kb_gate_kernel(tc, qT, kT, t, v, kb, og, out):
    nc = tc.nc
    with ExitStack() as ctx:
        sb = ctx.enter_context(tc.tile_pool(name="sb", bufs=1))
        ps = ctx.enter_context(tc.psum_pool(name="ps", bufs=1))
        ctx.enter_context(tc.manual_schedule())

        def tile(name, shape, dtype):
            return sb.tile(shape, dtype, name=name, align_bytes=64)

        def per_chunk(name, shape, dtype):
            return [tile("%s%d" % (name, c), shape, dtype) for c in range(CHUNKS)]

        warm = tile("warm", [P, 8], F32)
        t_sb = tile("t_sb", [P, PACK], F32)
        kb_sb = tile("kb_sb", [P, PACK], F32)
        k_raw = [tile("k_raw%d" % a, [P, PACK, N // 2], F32) for a in range(2)]
        k_grp = [[tile("k_grp%d%d" % (a, b), [P, 2, HALF, PACK], BF16) for b in range(2)] for a in range(2)]
        k_codes = tile("k_codes", [P, PACK, P], U32)
        k_scales = tile("k_scales", [P, PACK, P], U8)
        q_raw = per_chunk("q_raw", [P, PACK, QC], F32)
        q_grp = per_chunk("q_grp", [P, QC, PACK], BF16)
        q_codes = per_chunk("q_codes", [P, QC], U32)
        q_scales = per_chunk("q_scales", [P, QC], U8)
        v_raw = tile("v_raw", [P, H, PACK, E], F32)
        v_grp = tile("v_grp", [P, H, E, PACK], BF16)
        v_codes = tile("v_codes", [P, H, E], U32)
        v_scales = tile("v_scales", [P, H, E], U8)
        og_sb = tile("og_sb", [P, H, CHUNKS, E], F32)
        gate = per_chunk("gate", [P, H, E], F32)
        p_sb = per_chunk("p_sb", [P, PACK, H, QC], F32)
        w_grp = per_chunk("w_grp", [P, H, QC, PACK], BF16)
        w_codes = per_chunk("w_codes", [P, H, QC], U32)
        w_scales = per_chunk("w_scales", [P, H, QC], U8)
        res = per_chunk("res", [P, H, E], F32)

        s_ps = [[ps.tile([P, BANK], F32, name="s%d%d" % (h, b)) for b in range(3 - h)] for h in range(H)]
        y_ps = [ps.tile([P, 2, H, E], F32, name="y%d" % b) for b in range(3)]

        def y_view(c, hs):
            bank = 2 if (c, hs) == (CHUNKS - 1, slice(0, 1)) else c // 2
            return y_ps[bank][:, c % 2, hs].rearrange("p h e -> p (h e)")

        def score_view(c, h, r):
            bank = c % 2 if h == 1 else (r // 2 if c == 0 else (c + 1) % 3)
            return s_ps[h][bank][:, r * QC : (r + 1) * QC]

        def quantize(codes, scales, src):
            nc.vector.quantize_mx(out=codes.bitcast(FP8X4), scales=scales, in_=src)

        kT_v = kT.rearrange("h (p j) n -> (h p) j n", j=PACK)
        qT_v = qT.rearrange("h (p j) n -> (h p) j n", j=PACK)

        def load_k(a):
            nc.sync.dma_start(out=k_raw[a][:], in_=kT_v[:, :, a * (N // 2) : (a + 1) * (N // 2)])

        def load_q(c):
            nc.sync.dma_start(out=q_raw[c][:], in_=qT_v[:, :, c * QC : (c + 1) * QC])

        def load_v():
            nc.sync.dma_start(
                out=v_raw[:].rearrange("p h r e -> p h (r e)"), in_=v.rearrange("h (p r) e -> p h (r e)", r=PACK)
            )

        def load_og():
            nc.sync.dma_start(
                out=og_sb[:].rearrange("p h c e -> p (h c) e"), in_=og.rearrange("h (c p) e -> p (h c) e", p=P)
            )

        def load_small():
            nc.scalar.dma_start(out=kb_sb[:], in_=kb.rearrange("(p r) o -> p (r o)", r=PACK))
            nc.scalar.dma_start(out=t_sb[:], in_=t.rearrange("(p r) o -> p (r o)", r=PACK))

        def group_k(a, b, copy):
            src = k_raw[a][:].rearrange("p j (s r) -> p s j r", r=PACK)[:, :, :, 2 * b : 2 * b + 2]
            copy(out=k_grp[a][b][:].rearrange("p r s j -> p s j r"), in_=src)

        def quant_k(a, r):
            cols = slice(a * HALF, (a + 1) * HALF)
            quantize(k_codes[:, r, cols], k_scales[:, r, cols], k_grp[a][r // 2][:, r % 2].rearrange("p s j -> p (s j)"))

        def group_q(c, copy):
            copy(
                out=q_grp[c][:].rearrange("p (c i) j -> p c j i", i=RUN),
                in_=q_raw[c][:].rearrange("p j (c i) -> p c j i", i=RUN),
            )

        def quant_q(c):
            quantize(q_codes[c][:], q_scales[c][:], q_grp[c][:].rearrange("p q j -> p (q j)"))

        def group_v(h, on_vector=False):
            dst = v_grp[:, h].rearrange("p (c i) r -> p c r i", i=RUN)
            src = v_raw[:, h].rearrange("p r (c i) -> p c r i", i=RUN)
            if on_vector:
                nc.vector.tensor_scalar_mul(out=dst, in0=src, scalar1=OUT_SCALE)
            else:
                nc.scalar.activation(out=dst, in_=src, func=ACT.Copy, scale=OUT_SCALE)

        def quant_v(hs):
            quantize(
                v_codes[:, hs].rearrange("p h e -> p (h e)"),
                v_scales[:, hs].rearrange("p h e -> p (h e)"),
                v_grp[:, hs].rearrange("p h e r -> p (h e r)"),
            )

        def scores(c):
            pairs = [(r, h) for r in range(PACK) for h in range(H)]
            if c == 0:
                pairs = [(r, h) for h in range(H) for r in range(PACK)]
            for r, h in pairs:
                if True:
                    rows = slice(h * ROWS, (h + 1) * ROWS)
                    nc.tensor.matmul_mx(
                        out=score_view(c, h, r),
                        lhsT=k_codes[rows, r, :].bitcast(FP8X4),
                        lhsT_scale=k_scales[rows, r, :],
                        rhs=q_codes[c][rows, :].bitcast(FP8X4),
                        rhs_scale=q_scales[c][rows, :],
                        start=True,
                        stop=True,
                    )

        def silu(c, h, slots=range(PACK)):
            for r in slots:
                nc.scalar.activation(
                    out=p_sb[c][:, r, h], in_=score_view(c, h, r), func=ACT.Silu, bias=kb_sb[:, r : r + 1]
                )

        def weigh(c, hs):
            groups = (hs.stop - hs.start) * QC // RUN
            nc.vector.tensor_tensor(
                out=w_grp[c][:, hs].rearrange("p h (c i) r -> p (h c) r i", i=RUN),
                in0=p_sb[c][:, :, hs].rearrange("p r h (c i) -> p (h c) r i", i=RUN),
                in1=t_sb[:].unsqueeze(1).unsqueeze(3).to_broadcast([P, groups, PACK, RUN]),
                op=ALU.mult,
            )

        def quant_w(c, hs):
            quantize(
                w_codes[c][:, hs].rearrange("p h q -> p (h q)"),
                w_scales[c][:, hs].rearrange("p h q -> p (h q)"),
                w_grp[c][:, hs].rearrange("p h q r -> p (h q r)"),
            )

        def mix(c, hs):
            for h in range(hs.start, hs.stop):
                nc.tensor.matmul_mx(
                    out=y_view(c, slice(h, h + 1)),
                    lhsT=w_codes[c][:, h].bitcast(FP8X4),
                    lhsT_scale=w_scales[c][:, h],
                    rhs=v_codes[:, h].bitcast(FP8X4),
                    rhs_scale=v_scales[:, h],
                    start=True,
                    stop=True,
                )

        def half_tanh(c):
            nc.scalar.activation(out=gate[c][:], in_=og_sb[:, :, c], func=ACT.Tanh, scale=0.5)

        def finish(c, hs):
            nc.vector.scalar_tensor_tensor(
                out=res[c][:, hs].rearrange("p h e -> p (h e)"),
                in0=gate[c][:, hs].rearrange("p h e -> p (h e)"),
                scalar=1.0,
                in1=y_view(c, hs),
                op0=ALU.add,
                op1=ALU.mult,
            )
            nc.sync.dma_start(out=out[hs, c * QC : (c + 1) * QC].rearrange("h p e -> p h e"), in_=res[c][:, hs])

        vcopy = nc.vector.tensor_copy
        scopy = nc.scalar.copy
        H0, H1 = slice(0, 1), slice(1, 2)

        load_k(0)
        load_small()
        load_q(0)
        load_k(1)
        load_q(1)
        load_q(2)
        load_q(3)
        load_v()
        load_og()
        nc.vector.memset(warm[:], 0.0)
        nc.scalar.activation(out=warm[:, 4:5], in_=warm[:, 0:1], func=ACT.Silu)

        group_k(0, 0, vcopy)
        group_k(0, 1, scopy)
        quant_k(0, 0)
        quant_k(0, 1)
        quant_k(0, 2)
        quant_k(0, 3)
        group_q(0, vcopy)
        quant_q(0)
        group_k(1, 0, vcopy)
        group_k(1, 1, scopy)
        quant_k(1, 0)
        quant_k(1, 1)
        quant_k(1, 2)
        quant_k(1, 3)
        scores(0)
        group_q(1, vcopy)
        group_q(2, vcopy)
        quant_q(1)
        silu(0, 0)
        scores(1)
        quant_q(2)
        group_q(3, vcopy)
        silu(0, 1)
        weigh(0, H0)
        quant_q(3)
        scores(2)
        silu(1, 0)
        silu(1, 1)
        scores(3)
        silu(2, 0)
        weigh(0, H1)
        group_v(0, True)
        silu(2, 1)
        quant_w(0, BOTH)
        weigh(1, H0)
        weigh(1, H1)
        weigh(2, H0)
        quant_v(H0)
        weigh(2, H1)
        quant_w(1, BOTH)
        group_v(1)
        quant_v(H1)
        mix(0, BOTH)
        quant_w(2, BOTH)
        mix(1, BOTH)
        mix(2, BOTH)
        silu(3, 0)
        silu(3, 1)
        half_tanh(2)
        half_tanh(1)
        half_tanh(0)
        half_tanh(3)
        weigh(3, H0)
        weigh(3, H1)
        quant_w(3, H0)
        mix(3, H0)
        finish(2, BOTH)
        quant_w(3, H1)
        mix(3, H1)
        finish(1, BOTH)
        finish(0, BOTH)
        finish(3, H0)
        finish(3, H1)
